import numpy as np
import ml_dtypes


def mxq(x, axis, fmt="e4m3"):
    dtype, down = {"e4m3": (ml_dtypes.float8_e4m3fn, 7), "e5m2": (ml_dtypes.float8_e5m2, 14)}[fmt]
    v = np.moveaxis(np.asarray(x, np.float32).astype(ml_dtypes.bfloat16).astype(np.float64), axis, -1)
    blocks = v.reshape(v.shape[:-1] + (-1, 32))
    amax = np.abs(blocks).max(-1, keepdims=True)
    byte = np.maximum(np.where(amax > 0, np.frexp(amax)[1] - 1 + 127, 0) - down, 1)
    scale = np.exp2(byte - 127.0)
    codes = (blocks / scale).astype(np.float32).astype(dtype).astype(np.float64)
    return np.moveaxis((codes * scale).reshape(v.shape), -1, axis)


WIDE = False


def mx_kscale(k):
    if not WIDE:
        return np.ones(k)
    levels = np.array([10, -10, 5, -5, 0])
    if k % 512:
        return np.exp2(np.random.permutation(np.resize(levels, k // 32))).repeat(32)
    a = np.empty((k // 512, 16))
    for p in range(k // 512):
        a[p, :8] = np.random.permutation(np.resize(levels, 8))
        for g in range(8):
            far = levels[np.abs(levels - a[p, g]) >= 10]
            a[p, g + 8] = far[np.random.randint(len(far))]
    return np.exp2(a.ravel()).repeat(32)


def f64(x):
    return np.asarray(x).astype(np.float64)


def striped(idx):
    return np.tile(idx.reshape(-1, 16).T, (8, 1)).astype(np.uint16)


def unstriped(offs):
    return offs[:16].T.reshape(-1).astype(np.int64)


E2M1 = np.array([0.0, 0.5, 1.0, 1.5, 2.0, 3.0, 4.0, 6.0, -0.0, -0.5, -1.0, -1.5, -2.0, -3.0, -4.0, -6.0])


def pack_fp4(w):
    k, n = w.shape
    w = f64(np.asarray(w, np.float32).astype(ml_dtypes.bfloat16)).reshape(k // 32, 32, n)
    amax = np.abs(w).max(1)
    mant, ex = np.frexp(amax / 6.0)
    byte = np.clip(np.where(amax > 0, np.where(mant > 0.5, ex, ex - 1) + 127, 1), 1, 254)
    scaled = (w * np.exp2(127.0 - byte)[:, None, :]).reshape(k, n).astype(np.float32)
    c = np.ascontiguousarray(scaled.reshape(k // 512, 128, 4, n).transpose(0, 1, 3, 2)).astype(ml_dtypes.float4_e2m1fn).view(np.uint8) & 0xF
    words = (c[..., 0::2] | (c[..., 1::2] << 4)).reshape(k // 512, 128, 2 * n)
    return np.ascontiguousarray(words), np.ascontiguousarray(byte.astype(np.uint8).reshape(k // 512, 16, n))


def unpack_fp4(words, scales):
    g, _, n = scales.shape
    words = np.ascontiguousarray(words).reshape(g, 128, n, 2)
    nib = np.empty((g, 128, n, 4), np.uint8)
    nib[..., 0::2] = words & 0xF
    nib[..., 1::2] = words >> 4
    vals = E2M1[nib] * np.repeat(np.exp2(scales.astype(np.float64) - 127.0), 8, axis=1)[..., None]
    return vals.transpose(0, 1, 3, 2).reshape(g * 512, n)


def planes(y):
    n, m = y.shape
    v = y.astype(np.float32).astype(ml_dtypes.bfloat16).astype(np.float64).reshape(n // 32, 32, m)
    top = np.abs(v).max(1)
    byte = np.clip(np.where(top > 0, np.frexp(top)[1] - 1 + 127 - 7, 1), 1, 254)
    codes = (v * np.exp2(127.0 - byte)[:, None, :]).reshape(n, m).astype(np.float32).astype(ml_dtypes.float8_e4m3fn).view(np.uint8)
    words = codes.reshape(n // 512, 128, 4, m).transpose(0, 1, 3, 2)
    return np.ascontiguousarray(words), np.ascontiguousarray(byte.astype(np.uint8).reshape(n // 512, 16, m))


K, T, D, N = 1024, 1024, 3, 512
P = 2 ** 7


def setup_inputs():
    n = np.random.standard_normal
    s = mx_kscale(K)[:, None]
    packed_xT = pack_fp4(n((K, T)) * s)
    return {
        "x_words": packed_xT[0],
        "x_scales": packed_xT[1],
        "w1": (n((K, N)) / np.sqrt(K) / s).astype(np.float32),
        "score": np.tile(np.random.standard_normal((D, 1, T)), (1, P, 1)).astype(np.float32),
        "pos1": striped(np.random.permutation(T)),
        "pos2": striped(np.random.permutation(T)),
        "pos3": striped(np.random.permutation(T)),
    }


def reference(x_words, x_scales, w1, score, pos1, pos2, pos3):
    xq = unpack_fp4(x_words, x_scales)
    y = mxq(f64(w1), 0, "e4m3").T @ xq
    e0 = np.exp(f64(score)[0, :1])
    e1 = np.exp(f64(score)[1, :1])
    e2 = np.exp(f64(score)[2, :1])
    num = y[:, unstriped(pos1)] * e0 + y[:, unstriped(pos2)] * e1 + y[:, unstriped(pos3)] * e2
    den = e0 + e1 + e2
    out_0 = num / den
    return (out_0,) + planes(out_0)

@@ -1,0 +1,220 @@
+from contextlib import ExitStack
+
+import concourse.mybir as mybir
+from concourse.masks import make_identity
+
+K, T, D, N = 1024, 1024, 3, 512
+FLOPS = 2 * K * N * T
+BYTES = K * T // 2 + K * T // 32 + 4 * K * N + 4 * D * T + D * 128 * 64 * 2 + 4 * N * T + N * T + N * T // 32
+
+F32 = mybir.dt.float32
+BF16 = mybir.dt.bfloat16
+I32 = mybir.dt.int32
+U32 = mybir.dt.uint32
+U16 = mybir.dt.uint16
+U8 = mybir.dt.uint8
+FP8X4 = mybir.dt.float8_e4m3fn_x4
+FP4X4 = mybir.dt.float4_e2m1fn_x4
+ALU = mybir.AluOpType
+ACT = mybir.ActivationFunctionType
+AX = mybir.AxisListType
+
+P = 128
+PACK = 4
+PASSES = K // (P * PACK)
+BANK = 512
+BLOCKS = N // P
+VBLOCKS = T // P
+CHUNKS = (512, 256, 128, 128)
+
+
+def tile_picked_wgatv_none_lo_kernel(
+    tc, x_words, x_scales, w1, score, pos1, pos2, pos3, out_0, out_1, out_2
+):
+    nc = tc.nc
+    with ExitStack() as ctx:
+        keep = ctx.enter_context(tc.tile_pool(name="keep", bufs=1))
+        ring = ctx.enter_context(tc.tile_pool(name="ring", bufs=2))
+        gath = ctx.enter_context(tc.tile_pool(name="gath", bufs=6))
+        ps_mm = ctx.enter_context(tc.psum_pool(name="ps_mm", bufs=2))
+        ps_mid = ctx.enter_context(tc.psum_pool(name="ps_mid", bufs=2))
+        ps_fin = ctx.enter_context(tc.psum_pool(name="ps_fin", bufs=4))
+
+        x_sc = keep.tile([P, PASSES, T], U8, name="x_sc", align_bytes=64)
+        nc.gpsimd.memset(x_sc[:].bitcast(I32), 0)
+        zero = keep.tile([P, 1], F32, name="zero")
+        nc.vector.memset(zero[:], 0.0)
+        warm = keep.tile([P, 1], F32, name="warm")
+        nc.scalar.activation(warm[:], zero[:], ACT.Exp)
+        ident = keep.tile([P, P], F32, name="ident")
+        make_identity(nc, ident[:])
+
+        w_k = w1.rearrange("(g p j) m -> g p j m", g=PASSES, j=PACK)
+        w_raw = {}
+
+        def load_w(b0, nb):
+            for g in range(PASSES):
+                raw = keep.tile([P, PACK, nb * P], F32, name="w_raw_%d_%d" % (b0, g))
+                nc.sync.dma_start(out=raw[:], in_=w_k[g, :, :, b0 * P : (b0 + nb) * P])
+                for i in range(nb):
+                    w_raw[b0 + i, g] = raw[:, :, i * P : (i + 1) * P]
+
+        load_w(0, 1)
+        x_w = keep.tile([P, PASSES, 2 * T], U8, name="x_w", align_bytes=64)
+        nc.sync.dma_start(out=x_w[:].bitcast(I32), in_=x_words.rearrange("g p n -> p g n").bitcast(I32))
+        s_dc = keep.tile([P, D, VBLOCKS], F32, name="s_dc")
+        nc.sync.dma_start(out=s_dc[:], in_=score[:, 0, :].rearrange("d (p c) -> p d c", c=VBLOCKS))
+        for q in range(4):
+            nc.sync.dma_start(
+                out=x_sc[32 * q : 32 * q + 4, :, :].bitcast(I32),
+                in_=x_scales[:, 4 * q : 4 * q + 4, :].rearrange("g r n -> r g n").bitcast(I32),
+            )
+        lists = [keep.tile([P, T // 16], U16, name="list_%d" % d) for d in range(D)]
+        nc.sync.dma_start(lists[0][:], pos1)
+        load_w(1, 1)
+        nc.sync.dma_start(lists[1][:], pos2)
+        nc.sync.dma_start(lists[2][:], pos3)
+        load_w(2, 2)
+
+        top = keep.tile([P, VBLOCKS], F32, name="top")
+        nc.vector.tensor_reduce(top[:], s_dc[:].rearrange("p d c -> p c d"), AX.X, ALU.max)
+        diff = keep.tile([P, D, VBLOCKS], F32, name="diff")
+        nc.vector.tensor_tensor(diff[:], s_dc[:], top[:].unsqueeze(1).to_broadcast([P, D, VBLOCKS]), ALU.subtract)
+        expd = keep.tile([P, D, VBLOCKS], F32, name="expd")
+        nc.scalar.activation(expd[:], diff[:], ACT.Exp)
+        den = keep.tile([P, VBLOCKS], F32, name="den")
+        nc.vector.tensor_reduce(den[:], expd[:].rearrange("p d c -> p c d"), AX.X, ALU.add)
+        rec = keep.tile([P, VBLOCKS], F32, name="rec")
+        nc.vector.reciprocal(rec[:], den[:])
+        att = keep.tile([P, D, VBLOCKS], F32, name="att")
+        nc.vector.tensor_tensor(att[:], expd[:], rec[:].unsqueeze(1).to_broadcast([P, D, VBLOCKS]), ALU.mult)
+
+        att_rows = [keep.tile([P, T], F32, name="att_rows_%d" % d) for d in range(D)]
+
+        def spread(d):
+            for h in range(2):
+                a_ps = ps_fin.tile([P, BANK], F32, name="fin")
+                for i in range(4):
+                    c = 4 * h + i
+                    nc.tensor.transpose(a_ps[:, i * P : (i + 1) * P], att[:, d, c : c + 1].to_broadcast([P, P]), ident[:])
+                nc.scalar.copy(
+                    att_rows[d][:].rearrange("q (p c) -> q p c", c=VBLOCKS)[:, :, 4 * h : 4 * h + 4],
+                    a_ps[:].rearrange("q (c p) -> q p c", c=4),
+                )
+
+        y = [keep.tile([P, T], F32, name="y_%d" % b) for b in range(BLOCKS)]
+
+        def project(b):
+            w_bf = keep.tile([P, PASSES, P, PACK], BF16, name="w_bf_%d" % b, align_bytes=64)
+            w_q = keep.tile([P, PASSES, P], U32, name="w_q_%d" % b, align_bytes=64)
+            w_sc = keep.tile([P, PASSES, P], U8, name="w_sc_%d" % b, align_bytes=64)
+            for g in range(PASSES):
+                src = w_raw[b, g].rearrange("p j m -> p m j")
+                if b == 0:
+                    nc.vector.tensor_copy(w_bf[:, g], src)
+                else:
+                    nc.scalar.copy(w_bf[:, g], src)
+            if b == 0:
+                for g in range(PASSES):
+                    nc.vector.quantize_mx(w_q[:, g, :].bitcast(FP8X4), w_sc[:, g, :], w_bf[:, g].rearrange("p m j -> p (m j)"))
+            else:
+                nc.vector.quantize_mx(
+                    w_q[:].rearrange("p g m -> p (g m)").bitcast(FP8X4),
+                    w_sc[:].rearrange("p g m -> p (g m)"),
+                    w_bf[:].rearrange("p g m j -> p (g m j)"),
+                )
+            for h in range(T // BANK):
+                acc = ps_mm.tile([P, BANK], F32, name="acc")
+                for g in range(PASSES):
+                    nc.tensor.matmul_mx(
+                        acc[:],
+                        lhsT=w_q[:, g, :].bitcast(FP8X4),
+                        lhsT_scale=w_sc[:, g, :],
+                        rhs=x_w[:, g, 2 * h * BANK : 2 * (h + 1) * BANK].bitcast(FP4X4),
+                        rhs_scale=x_sc[:, g, h * BANK : (h + 1) * BANK],
+                        start=(g == 0),
+                        stop=(g == PASSES - 1),
+                    )
+                if b == 0 and h == 1:
+                    nc.vector.tensor_copy(y[b][:, h * BANK : (h + 1) * BANK], acc[:])
+                else:
+                    nc.scalar.copy(y[b][:, h * BANK : (h + 1) * BANK], acc[:])
+
+        o_q = keep.tile([P, T], U32, name="o_q", align_bytes=64)
+        o_sc = keep.tile([P, T], U8, name="o_sc", align_bytes=64)
+        out_rows = out_0.rearrange("(p t) v -> p t v", t=PACK)
+        out_words = out_1[0].rearrange("p c r -> p (c r)").bitcast(I32)
+
+        def gather_block(v0, width, b, mid):
+            nv = width // P
+            terms = []
+            for d in range(D):
+                term = gath.tile([P, BANK], F32, name="term")
+                nc.vector.tensor_tensor(
+                    term[:, 0:width],
+                    y[b][:].indirect(lists[d][:, v0 // 16 : (v0 + width) // 16]),
+                    att_rows[d][:, v0 : v0 + width],
+                    ALU.mult,
+                )
+                terms.append(term)
+            m_ps = ps_mid.tile([P, BANK], F32, name="m_ps")
+            for i in range(nv):
+                for d in range(D):
+                    nc.tensor.matmul(
+                        m_ps[:, i * P : (i + 1) * P],
+                        lhsT=terms[d][:, i * P : (i + 1) * P],
+                        rhs=ident[:],
+                        start=(d == 0),
+                        stop=(d == D - 1),
+                        is_transpose=True,
+                    )
+            nc.scalar.copy(
+                mid[:, 0:nv, :, 32 * b : 32 * (b + 1)],
+                m_ps[:, 0:width].rearrange("v (i q t) -> v i t q", i=nv, t=PACK),
+            )
+
+        def finish(v0, width, mid, last):
+            nv = width // P
+            o_f = ring.tile([P, PACK, width], F32, name="o_f")
+            o_bf = ring.tile([P, width, PACK], BF16, name="o_bf", align_bytes=64)
+            for i in range(nv):
+                f_ps = ps_fin.tile([P, BANK], F32, name="fin")
+                for t in range(PACK):
+                    nc.tensor.transpose(f_ps[:, t * P : (t + 1) * P], mid[:, i, t, :], ident[:])
+                f_tv = f_ps[:].rearrange("p (t v) -> p t v", t=PACK)
+                if last:
+                    nc.vector.tensor_copy(o_bf[:, i * P : (i + 1) * P, :], f_tv.rearrange("p t v -> p v t"))
+                    f_ps = ps_fin.tile([P, BANK], F32, name="fin")
+                    for t in range(PACK):
+                        nc.tensor.transpose(f_ps[:, t * P : (t + 1) * P], mid[:, i, t, :], ident[:])
+                    f_tv = f_ps[:].rearrange("p (t v) -> p t v", t=PACK)
+                else:
+                    nc.scalar.copy(o_bf[:, i * P : (i + 1) * P, :], f_tv.rearrange("p t v -> p v t"))
+                nc.scalar.copy(o_f[:, :, i * P : (i + 1) * P], f_tv)
+            nc.sync.dma_start(out=out_rows[:, :, v0 : v0 + width], in_=o_f[:])
+            nc.vector.quantize_mx(
+                o_q[:, v0 : v0 + width].bitcast(FP8X4),
+                o_sc[:, v0 : v0 + width],
+                o_bf[:].rearrange("p v t -> p (v t)"),
+            )
+            nc.sync.dma_start(out=out_words[:, v0 : v0 + width], in_=o_q[:, v0 : v0 + width].bitcast(I32))
+
+        spread(0)
+        project(0)
+        spread(1)
+        spread(2)
+        project(1)
+        v0 = 0
+        for n, width in enumerate(CHUNKS):
+            mid = ring.tile([P, 4, PACK, P], F32, name="mid")
+            for b in range(BLOCKS):
+                gather_block(v0, width, b, mid)
+                if n == 0 and b + 2 < BLOCKS:
+                    project(b + 2)
+            finish(v0, width, mid, n == len(CHUNKS) - 1)
+            v0 = v0 + width
+        for q in range(4):
+            nc.sync.dma_start(
+                out=out_2[0, 4 * q : 4 * q + 4, :].bitcast(I32),
+                in_=o_sc[32 * q : 32 * q + 4, :].bitcast(I32),
+            )

@@ -25,7 +25,8 @@ PASSES = K // (P * PACK)
 BANK = 512
 BLOCKS = N // P
 VBLOCKS = T // P
-CHUNKS = (512, 256, 128, 128)
+CHUNKS = (384, 256, 256, 128)
+SPARE = 16
 
 
 def tile_picked_wgatv_none_lo_kernel(
@@ -36,9 +37,11 @@ def tile_picked_wgatv_none_lo_kernel(
         keep = ctx.enter_context(tc.tile_pool(name="keep", bufs=1))
         ring = ctx.enter_context(tc.tile_pool(name="ring", bufs=2))
         gath = ctx.enter_context(tc.tile_pool(name="gath", bufs=6))
-        ps_mm = ctx.enter_context(tc.psum_pool(name="ps_mm", bufs=2))
-        ps_mid = ctx.enter_context(tc.psum_pool(name="ps_mid", bufs=2))
-        ps_fin = ctx.enter_context(tc.psum_pool(name="ps_fin", bufs=4))
+        psum = ctx.enter_context(tc.psum_pool(name="psum", bufs=1))
+
+        def bank(k):
+            return psum.tile([P, BANK], F32, name="bank_%d" % k)
+
 
         x_sc = keep.tile([P, PASSES, T], U8, name="x_sc", align_bytes=64)
         nc.gpsimd.memset(x_sc[:].bitcast(I32), 0)
@@ -52,169 +55,203 @@ def tile_picked_wgatv_none_lo_kernel(
         w_k = w1.rearrange("(g p j) m -> g p j m", g=PASSES, j=PACK)
         w_raw = {}
 
-        def load_w(b0, nb):
-            for g in range(PASSES):
+        def load_w(b0, nb, passes):
+            for g in passes:
                 raw = keep.tile([P, PACK, nb * P], F32, name="w_raw_%d_%d" % (b0, g))
                 nc.sync.dma_start(out=raw[:], in_=w_k[g, :, :, b0 * P : (b0 + nb) * P])
                 for i in range(nb):
                     w_raw[b0 + i, g] = raw[:, :, i * P : (i + 1) * P]
 
-        load_w(0, 1)
-        x_w = keep.tile([P, PASSES, 2 * T], U8, name="x_w", align_bytes=64)
-        nc.sync.dma_start(out=x_w[:].bitcast(I32), in_=x_words.rearrange("g p n -> p g n").bitcast(I32))
-        s_dc = keep.tile([P, D, VBLOCKS], F32, name="s_dc")
-        nc.sync.dma_start(out=s_dc[:], in_=score[:, 0, :].rearrange("d (p c) -> p d c", c=VBLOCKS))
+        load_w(0, 1, [0])
+        s_pad = keep.tile([P, D, 2, 8], F32, name="s_pad")
+        s_dc = s_pad[:, :, :, 0:4]
+        nc.sync.dma_start(
+            out=s_pad[:].rearrange("p d h i -> p (d h) i")[:, :, 0:4],
+            in_=score.rearrange("d r (h p i) -> p (d r h) i", h=2, i=4)[:, 0 : 5 * 129 + 1 : 129, :],
+        )
         for q in range(4):
             nc.sync.dma_start(
                 out=x_sc[32 * q : 32 * q + 4, :, :].bitcast(I32),
                 in_=x_scales[:, 4 * q : 4 * q + 4, :].rearrange("g r n -> r g n").bitcast(I32),
             )
+        x_w = keep.tile([P, PASSES, 2 * T], U8, name="x_w", align_bytes=64)
+        nc.sync.dma_start(out=x_w[:].bitcast(I32), in_=x_words.rearrange("g p n -> p g n").bitcast(I32))
+        load_w(0, 1, [1])
         lists = [keep.tile([P, T // 16], U16, name="list_%d" % d) for d in range(D)]
         nc.sync.dma_start(lists[0][:], pos1)
-        load_w(1, 1)
         nc.sync.dma_start(lists[1][:], pos2)
         nc.sync.dma_start(lists[2][:], pos3)
-        load_w(2, 2)
+        load_w(1, 3, range(PASSES))
 
         top = keep.tile([P, VBLOCKS], F32, name="top")
-        nc.vector.tensor_reduce(top[:], s_dc[:].rearrange("p d c -> p c d"), AX.X, ALU.max)
+        top_hi = top[:].rearrange("p (h i) -> p h i", h=2)
+        nc.vector.tensor_reduce(top_hi, s_dc.rearrange("p d h i -> p h i d"), AX.X, ALU.max)
         diff = keep.tile([P, D, VBLOCKS], F32, name="diff")
-        nc.vector.tensor_tensor(diff[:], s_dc[:], top[:].unsqueeze(1).to_broadcast([P, D, VBLOCKS]), ALU.subtract)
+        nc.vector.tensor_tensor(
+            diff[:].rearrange("p d (h i) -> p d h i", h=2),
+            s_dc,
+            top_hi.unsqueeze(1).to_broadcast([P, D, 2, 4]),
+            ALU.subtract,
+        )
         expd = keep.tile([P, D, VBLOCKS], F32, name="expd")
         nc.scalar.activation(expd[:], diff[:], ACT.Exp)
         den = keep.tile([P, VBLOCKS], F32, name="den")
         nc.vector.tensor_reduce(den[:], expd[:].rearrange("p d c -> p c d"), AX.X, ALU.add)
         rec = keep.tile([P, VBLOCKS], F32, name="rec")
         nc.vector.reciprocal(rec[:], den[:])
-        att = keep.tile([P, D, VBLOCKS], F32, name="att")
+        att = keep.tile([P, D, VBLOCKS], F32, name="stage_1", align_bytes=64)
         nc.vector.tensor_tensor(att[:], expd[:], rec[:].unsqueeze(1).to_broadcast([P, D, VBLOCKS]), ALU.mult)
 
         att_rows = [keep.tile([P, T], F32, name="att_rows_%d" % d) for d in range(D)]
 
         def spread(d):
             for h in range(2):
-                a_ps = ps_fin.tile([P, BANK], F32, name="fin")
+                a_ps = bank(4 + h) if d == 0 else bank(6 + h)
                 for i in range(4):
                     c = 4 * h + i
                     nc.tensor.transpose(a_ps[:, i * P : (i + 1) * P], att[:, d, c : c + 1].to_broadcast([P, P]), ident[:])
                 nc.scalar.copy(
-                    att_rows[d][:].rearrange("q (p c) -> q p c", c=VBLOCKS)[:, :, 4 * h : 4 * h + 4],
+                    att_rows[d][:, h * BANK : (h + 1) * BANK].rearrange("q (p c) -> q p c", c=4),
                     a_ps[:].rearrange("q (c p) -> q p c", c=4),
                 )
 
-        y = [keep.tile([P, T], F32, name="y_%d" % b) for b in range(BLOCKS)]
+        y = [keep.tile([P, T + SPARE], F32, name="y_%d" % b) for b in range(BLOCKS)]
+        for b in range(BLOCKS):
+            nc.gpsimd.memset(y[b][:, T:], 0.0)
 
         def project(b):
-            w_bf = keep.tile([P, PASSES, P, PACK], BF16, name="w_bf_%d" % b, align_bytes=64)
             w_q = keep.tile([P, PASSES, P], U32, name="w_q_%d" % b, align_bytes=64)
             w_sc = keep.tile([P, PASSES, P], U8, name="w_sc_%d" % b, align_bytes=64)
-            for g in range(PASSES):
-                src = w_raw[b, g].rearrange("p j m -> p m j")
-                if b == 0:
-                    nc.vector.tensor_copy(w_bf[:, g], src)
-                else:
-                    nc.scalar.copy(w_bf[:, g], src)
+            accs = [bank(6 + h) for h in range(T // BANK)]
+
+            def mm(g, h):
+                nc.tensor.matmul_mx(
+                    accs[h][:],
+                    lhsT=w_q[:, g, :].bitcast(FP8X4),
+                    lhsT_scale=w_sc[:, g, :],
+                    rhs=x_w[:, g, 2 * h * BANK : 2 * (h + 1) * BANK].bitcast(FP4X4),
+                    rhs_scale=x_sc[:, g, h * BANK : (h + 1) * BANK],
+                    start=(g == 0),
+                    stop=(g == PASSES - 1),
+                )
+
             if b == 0:
                 for g in range(PASSES):
-                    nc.vector.quantize_mx(w_q[:, g, :].bitcast(FP8X4), w_sc[:, g, :], w_bf[:, g].rearrange("p m j -> p (m j)"))
+                    w_bf = keep.tile([P, P, PACK], BF16, name="w_bf_first_%d" % g, align_bytes=64)
+                    nc.vector.tensor_copy(w_bf[:], w_raw[b, g].rearrange("p j m -> p m j"))
+                    nc.vector.quantize_mx(w_q[:, g, :].bitcast(FP8X4), w_sc[:, g, :], w_bf[:].rearrange("p m j -> p (m j)"))
+                    for h in range(T // BANK):
+                        mm(g, h)
+                nc.scalar.copy(y[b][:, 0:BANK], accs[0][:])
+                nc.vector.tensor_copy(y[b][:, BANK:T], accs[1][:])
             else:
+                w_bf = keep.tile([P, PASSES, P, PACK], BF16, name="stage_%d" % b, align_bytes=64)
+                for g in range(PASSES):
+                    nc.scalar.copy(w_bf[:, g], w_raw[b, g].rearrange("p j m -> p m j"))
                 nc.vector.quantize_mx(
                     w_q[:].rearrange("p g m -> p (g m)").bitcast(FP8X4),
                     w_sc[:].rearrange("p g m -> p (g m)"),
                     w_bf[:].rearrange("p g m j -> p (g m j)"),
                 )
-            for h in range(T // BANK):
-                acc = ps_mm.tile([P, BANK], F32, name="acc")
-                for g in range(PASSES):
-                    nc.tensor.matmul_mx(
-                        acc[:],
-                        lhsT=w_q[:, g, :].bitcast(FP8X4),
-                        lhsT_scale=w_sc[:, g, :],
-                        rhs=x_w[:, g, 2 * h * BANK : 2 * (h + 1) * BANK].bitcast(FP4X4),
-                        rhs_scale=x_sc[:, g, h * BANK : (h + 1) * BANK],
-                        start=(g == 0),
-                        stop=(g == PASSES - 1),
-                    )
-                if b == 0 and h == 1:
-                    nc.vector.tensor_copy(y[b][:, h * BANK : (h + 1) * BANK], acc[:])
-                else:
-                    nc.scalar.copy(y[b][:, h * BANK : (h + 1) * BANK], acc[:])
+                for h in range(T // BANK):
+                    for g in range(PASSES):
+                        mm(g, h)
+                    nc.scalar.copy(y[b][:, h * BANK : (h + 1) * BANK], accs[h][:])
 
         o_q = keep.tile([P, T], U32, name="o_q", align_bytes=64)
         o_sc = keep.tile([P, T], U8, name="o_sc", align_bytes=64)
         out_rows = out_0.rearrange("(p t) v -> p t v", t=PACK)
         out_words = out_1[0].rearrange("p c r -> p (c r)").bitcast(I32)
 
-        def gather_block(v0, width, b, mid):
-            nv = width // P
-            terms = []
-            for d in range(D):
-                term = gath.tile([P, BANK], F32, name="term")
-                nc.vector.tensor_tensor(
-                    term[:, 0:width],
-                    y[b][:].indirect(lists[d][:, v0 // 16 : (v0 + width) // 16]),
-                    att_rows[d][:, v0 : v0 + width],
-                    ALU.mult,
-                )
-                terms.append(term)
-            m_ps = ps_mid.tile([P, BANK], F32, name="m_ps")
-            for i in range(nv):
-                for d in range(D):
-                    nc.tensor.matmul(
-                        m_ps[:, i * P : (i + 1) * P],
-                        lhsT=terms[d][:, i * P : (i + 1) * P],
-                        rhs=ident[:],
-                        start=(d == 0),
-                        stop=(d == D - 1),
-                        is_transpose=True,
-                    )
-            nc.scalar.copy(
-                mid[:, 0:nv, :, 32 * b : 32 * (b + 1)],
-                m_ps[:, 0:width].rearrange("v (i q t) -> v i t q", i=nv, t=PACK),
-            )
+        starts = [sum(CHUNKS[:n]) for n in range(len(CHUNKS))]
+        mids = [keep.tile([P, PACK, P], F32, name="mid_%d" % c, align_bytes=64) for c in range(VBLOCKS)]
 
-        def finish(v0, width, mid, last):
-            nv = width // P
+        def gather(b, d, v0, width, banks, tag=None):
+            if tag is None:
+                term = gath.tile([P, width], F32, name="term")
+            else:
+                term = keep.tile([P, width], F32, name=tag, align_bytes=64)
+            nc.vector.tensor_tensor(
+                term[:],
+                y[b][:].indirect(lists[d][:, v0 // 16 : (v0 + width) // 16]),
+                att_rows[d][:, v0 : v0 + width],
+                ALU.mult,
+            )
+            per_bank = min(width, BANK) // P
+            for i in range(width // P):
+                j = i % per_bank
+                nc.tensor.matmul(
+                    banks[i // per_bank][:, j * P : (j + 1) * P],
+                    lhsT=term[:, i * P : (i + 1) * P],
+                    rhs=ident[:],
+                    start=(d == 0 and j == 0),
+                    stop=(d == D - 1 and j == per_bank - 1),
+                    is_transpose=True,
+                )
+
+        def to_mid(b, v0, sums):
+            for i in range(sums.shape[1] // P):
+                c = v0 // P + i
+                copy = nc.vector.tensor_copy if (b, c) == (BLOCKS - 1, VBLOCKS - 1) else nc.scalar.copy
+                copy(
+                    mids[c][:, :, 32 * b : 32 * (b + 1)],
+                    sums[:, i * P : (i + 1) * P].rearrange("v (q t) -> v t q", t=PACK),
+                )
+
+        def whole_block(b, tags, between):
+            banks = [bank(2 * b + h) for h in range(T // BANK)]
+            for d in range(D):
+                if b == 0 and d == 0:
+                    gather(b, d, 0, BANK, banks[0:1], tags[d])
+                    gather(b, d, BANK, BANK, banks[1:2])
+                else:
+                    gather(b, d, 0, T, banks, tags[d])
+                between[d]()
+            for h, sums in enumerate(banks):
+                to_mid(b, h * BANK, sums[:])
+
+        def finish(n):
+            v0, width = starts[n], CHUNKS[n]
+            last = n >= len(CHUNKS) - 2
             o_f = ring.tile([P, PACK, width], F32, name="o_f")
             o_bf = ring.tile([P, width, PACK], BF16, name="o_bf", align_bytes=64)
-            for i in range(nv):
-                f_ps = ps_fin.tile([P, BANK], F32, name="fin")
+            for i in range(width // P):
+                f_ps = bank(4 + (v0 // P + i) % 4)
                 for t in range(PACK):
-                    nc.tensor.transpose(f_ps[:, t * P : (t + 1) * P], mid[:, i, t, :], ident[:])
+                    nc.tensor.transpose(f_ps[:, t * P : (t + 1) * P], mids[v0 // P + i][:, t, :], ident[:])
                 f_tv = f_ps[:].rearrange("p (t v) -> p t v", t=PACK)
-                if last:
-                    nc.vector.tensor_copy(o_bf[:, i * P : (i + 1) * P, :], f_tv.rearrange("p t v -> p v t"))
-                    f_ps = ps_fin.tile([P, BANK], F32, name="fin")
-                    for t in range(PACK):
-                        nc.tensor.transpose(f_ps[:, t * P : (t + 1) * P], mid[:, i, t, :], ident[:])
-                    f_tv = f_ps[:].rearrange("p (t v) -> p t v", t=PACK)
-                else:
-                    nc.scalar.copy(o_bf[:, i * P : (i + 1) * P, :], f_tv.rearrange("p t v -> p v t"))
                 nc.scalar.copy(o_f[:, :, i * P : (i + 1) * P], f_tv)
+                if not last:
+                    nc.scalar.copy(o_bf[:, i * P : (i + 1) * P, :], f_tv.rearrange("p t v -> p v t"))
             nc.sync.dma_start(out=out_rows[:, :, v0 : v0 + width], in_=o_f[:])
-            nc.vector.quantize_mx(
-                o_q[:, v0 : v0 + width].bitcast(FP8X4),
-                o_sc[:, v0 : v0 + width],
-                o_bf[:].rearrange("p v t -> p (v t)"),
-            )
+            if last:
+                nc.vector.tensor_copy(o_bf[:], o_f[:].rearrange("p t v -> p v t"))
+            for c0 in range(0, width, 2 * P):
+                c1 = min(c0 + 2 * P, width)
+                nc.vector.quantize_mx(
+                    o_q[:, v0 + c0 : v0 + c1].bitcast(FP8X4),
+                    o_sc[:, v0 + c0 : v0 + c1],
+                    o_bf[:, c0:c1, :].rearrange("p v t -> p (v t)"),
+                )
             nc.sync.dma_start(out=out_words[:, v0 : v0 + width], in_=o_q[:, v0 : v0 + width].bitcast(I32))
 
         spread(0)
         project(0)
         spread(1)
         spread(2)
-        project(1)
-        v0 = 0
+        whole_block(0, ("stage_2", "stage_3", "stage_1"), (lambda: None, lambda: project(1), lambda: project(2)))
+        whole_block(1, ("stage_2", None, "stage_3"), (lambda: None, lambda: project(3), lambda: None))
         for n, width in enumerate(CHUNKS):
-            mid = ring.tile([P, 4, PACK, P], F32, name="mid")
-            for b in range(BLOCKS):
-                gather_block(v0, width, b, mid)
-                if n == 0 and b + 2 < BLOCKS:
-                    project(b + 2)
-            finish(v0, width, mid, n == len(CHUNKS) - 1)
-            v0 = v0 + width
+            for b in range(2, BLOCKS):
+                sums = bank(2 * (n % 2) + b - 2)
+                for d in range(D):
+                    held = n > 0 and (b, d) == (BLOCKS - 1, D - 1)
+                    gather(b, d, starts[n], width, [sums], "mid_%d" % (starts[n - 1] // P) if held else None)
+                to_mid(b, starts[n], sums[:, 0:width])
+            finish(n)
         for q in range(4):
-            nc.sync.dma_start(
+            queue = nc.sync if q % 2 == 0 else nc.scalar
+            queue.dma_start(
                 out=out_2[0, 4 * q : 4 * q + 4, :].bitcast(I32),
                 in_=o_sc[32 * q : 32 * q + 4, :].bitcast(I32),
             )

from contextlib import ExitStack

import concourse.mybir as mybir
from concourse.masks import make_identity

K, T, D, N = 1024, 1024, 3, 512
FLOPS = 2 * K * N * T
BYTES = K * T // 2 + K * T // 32 + 4 * K * N + 4 * D * T + D * 128 * 64 * 2 + 4 * N * T + N * T + N * T // 32

F32 = mybir.dt.float32
BF16 = mybir.dt.bfloat16
I32 = mybir.dt.int32
U32 = mybir.dt.uint32
U16 = mybir.dt.uint16
U8 = mybir.dt.uint8
FP8X4 = mybir.dt.float8_e4m3fn_x4
FP4X4 = mybir.dt.float4_e2m1fn_x4
ALU = mybir.AluOpType
ACT = mybir.ActivationFunctionType
AX = mybir.AxisListType

P = 128
PACK = 4
PASSES = K // (P * PACK)
BANK = 512
BLOCKS = N // P
VBLOCKS = T // P
CHUNKS = (384, 256, 256, 128)
SPARE = 16


def tile_picked_wgatv_none_lo_kernel(
    tc, x_words, x_scales, w1, score, pos1, pos2, pos3, out_0, out_1, out_2
):
    nc = tc.nc
    with ExitStack() as ctx:
        keep = ctx.enter_context(tc.tile_pool(name="keep", bufs=1))
        ring = ctx.enter_context(tc.tile_pool(name="ring", bufs=2))
        gath = ctx.enter_context(tc.tile_pool(name="gath", bufs=6))
        psum = ctx.enter_context(tc.psum_pool(name="psum", bufs=1))

        def bank(k):
            return psum.tile([P, BANK], F32, name="bank_%d" % k)


        x_sc = keep.tile([P, PASSES, T], U8, name="x_sc", align_bytes=64)
        nc.gpsimd.memset(x_sc[:].bitcast(I32), 0)
        zero = keep.tile([P, 1], F32, name="zero")
        nc.vector.memset(zero[:], 0.0)
        warm = keep.tile([P, 1], F32, name="warm")
        nc.scalar.activation(warm[:], zero[:], ACT.Exp)
        ident = keep.tile([P, P], F32, name="ident")
        make_identity(nc, ident[:])

        w_k = w1.rearrange("(g p j) m -> g p j m", g=PASSES, j=PACK)
        w_raw = {}

        def load_w(b0, nb, passes):
            for g in passes:
                raw = keep.tile([P, PACK, nb * P], F32, name="w_raw_%d_%d" % (b0, g))
                nc.sync.dma_start(out=raw[:], in_=w_k[g, :, :, b0 * P : (b0 + nb) * P])
                for i in range(nb):
                    w_raw[b0 + i, g] = raw[:, :, i * P : (i + 1) * P]

        load_w(0, 1, [0])
        s_pad = keep.tile([P, D, 2, 8], F32, name="s_pad")
        s_dc = s_pad[:, :, :, 0:4]
        nc.sync.dma_start(
            out=s_pad[:].rearrange("p d h i -> p (d h) i")[:, :, 0:4],
            in_=score.rearrange("d r (h p i) -> p (d r h) i", h=2, i=4)[:, 0 : 5 * 129 + 1 : 129, :],
        )
        for q in range(4):
            nc.sync.dma_start(
                out=x_sc[32 * q : 32 * q + 4, :, :].bitcast(I32),
                in_=x_scales[:, 4 * q : 4 * q + 4, :].rearrange("g r n -> r g n").bitcast(I32),
            )
        x_w = keep.tile([P, PASSES, 2 * T], U8, name="x_w", align_bytes=64)
        nc.sync.dma_start(out=x_w[:].bitcast(I32), in_=x_words.rearrange("g p n -> p g n").bitcast(I32))
        load_w(0, 1, [1])
        lists = [keep.tile([P, T // 16], U16, name="list_%d" % d) for d in range(D)]
        nc.sync.dma_start(lists[0][:], pos1)
        nc.sync.dma_start(lists[1][:], pos2)
        nc.sync.dma_start(lists[2][:], pos3)
        load_w(1, 3, range(PASSES))

        top = keep.tile([P, VBLOCKS], F32, name="top")
        top_hi = top[:].rearrange("p (h i) -> p h i", h=2)
        nc.vector.tensor_reduce(top_hi, s_dc.rearrange("p d h i -> p h i d"), AX.X, ALU.max)
        diff = keep.tile([P, D, VBLOCKS], F32, name="diff")
        nc.vector.tensor_tensor(
            diff[:].rearrange("p d (h i) -> p d h i", h=2),
            s_dc,
            top_hi.unsqueeze(1).to_broadcast([P, D, 2, 4]),
            ALU.subtract,
        )
        expd = keep.tile([P, D, VBLOCKS], F32, name="expd")
        nc.scalar.activation(expd[:], diff[:], ACT.Exp)
        den = keep.tile([P, VBLOCKS], F32, name="den")
        nc.vector.tensor_reduce(den[:], expd[:].rearrange("p d c -> p c d"), AX.X, ALU.add)
        rec = keep.tile([P, VBLOCKS], F32, name="rec")
        nc.vector.reciprocal(rec[:], den[:])
        att = keep.tile([P, D, VBLOCKS], F32, name="stage_1", align_bytes=64)
        nc.vector.tensor_tensor(att[:], expd[:], rec[:].unsqueeze(1).to_broadcast([P, D, VBLOCKS]), ALU.mult)

        att_rows = [keep.tile([P, T], F32, name="att_rows_%d" % d) for d in range(D)]

        def spread(d):
            for h in range(2):
                a_ps = bank(4 + h) if d == 0 else bank(6 + h)
                for i in range(4):
                    c = 4 * h + i
                    nc.tensor.transpose(a_ps[:, i * P : (i + 1) * P], att[:, d, c : c + 1].to_broadcast([P, P]), ident[:])
                nc.scalar.copy(
                    att_rows[d][:, h * BANK : (h + 1) * BANK].rearrange("q (p c) -> q p c", c=4),
                    a_ps[:].rearrange("q (c p) -> q p c", c=4),
                )

        y = [keep.tile([P, T + SPARE], F32, name="y_%d" % b) for b in range(BLOCKS)]
        for b in range(BLOCKS):
            nc.gpsimd.memset(y[b][:, T:], 0.0)

        def project(b):
            w_q = keep.tile([P, PASSES, P], U32, name="w_q_%d" % b, align_bytes=64)
            w_sc = keep.tile([P, PASSES, P], U8, name="w_sc_%d" % b, align_bytes=64)
            accs = [bank(6 + h) for h in range(T // BANK)]

            def mm(g, h):
                nc.tensor.matmul_mx(
                    accs[h][:],
                    lhsT=w_q[:, g, :].bitcast(FP8X4),
                    lhsT_scale=w_sc[:, g, :],
                    rhs=x_w[:, g, 2 * h * BANK : 2 * (h + 1) * BANK].bitcast(FP4X4),
                    rhs_scale=x_sc[:, g, h * BANK : (h + 1) * BANK],
                    start=(g == 0),
                    stop=(g == PASSES - 1),
                )

            if b == 0:
                for g in range(PASSES):
                    w_bf = keep.tile([P, P, PACK], BF16, name="w_bf_first_%d" % g, align_bytes=64)
                    nc.vector.tensor_copy(w_bf[:], w_raw[b, g].rearrange("p j m -> p m j"))
                    nc.vector.quantize_mx(w_q[:, g, :].bitcast(FP8X4), w_sc[:, g, :], w_bf[:].rearrange("p m j -> p (m j)"))
                    for h in range(T // BANK):
                        mm(g, h)
                nc.scalar.copy(y[b][:, 0:BANK], accs[0][:])
                nc.vector.tensor_copy(y[b][:, BANK:T], accs[1][:])
            else:
                w_bf = keep.tile([P, PASSES, P, PACK], BF16, name="stage_%d" % b, align_bytes=64)
                for g in range(PASSES):
                    nc.scalar.copy(w_bf[:, g], w_raw[b, g].rearrange("p j m -> p m j"))
                nc.vector.quantize_mx(
                    w_q[:].rearrange("p g m -> p (g m)").bitcast(FP8X4),
                    w_sc[:].rearrange("p g m -> p (g m)"),
                    w_bf[:].rearrange("p g m j -> p (g m j)"),
                )
                for h in range(T // BANK):
                    for g in range(PASSES):
                        mm(g, h)
                    nc.scalar.copy(y[b][:, h * BANK : (h + 1) * BANK], accs[h][:])

        o_q = keep.tile([P, T], U32, name="o_q", align_bytes=64)
        o_sc = keep.tile([P, T], U8, name="o_sc", align_bytes=64)
        out_rows = out_0.rearrange("(p t) v -> p t v", t=PACK)
        out_words = out_1[0].rearrange("p c r -> p (c r)").bitcast(I32)

        starts = [sum(CHUNKS[:n]) for n in range(len(CHUNKS))]
        mids = [keep.tile([P, PACK, P], F32, name="mid_%d" % c, align_bytes=64) for c in range(VBLOCKS)]

        def gather(b, d, v0, width, banks, tag=None):
            if tag is None:
                term = gath.tile([P, width], F32, name="term")
            else:
                term = keep.tile([P, width], F32, name=tag, align_bytes=64)
            nc.vector.tensor_tensor(
                term[:],
                y[b][:].indirect(lists[d][:, v0 // 16 : (v0 + width) // 16]),
                att_rows[d][:, v0 : v0 + width],
                ALU.mult,
            )
            per_bank = min(width, BANK) // P
            for i in range(width // P):
                j = i % per_bank
                nc.tensor.matmul(
                    banks[i // per_bank][:, j * P : (j + 1) * P],
                    lhsT=term[:, i * P : (i + 1) * P],
                    rhs=ident[:],
                    start=(d == 0 and j == 0),
                    stop=(d == D - 1 and j == per_bank - 1),
                    is_transpose=True,
                )

        def to_mid(b, v0, sums):
            for i in range(sums.shape[1] // P):
                c = v0 // P + i
                copy = nc.vector.tensor_copy if (b, c) == (BLOCKS - 1, VBLOCKS - 1) else nc.scalar.copy
                copy(
                    mids[c][:, :, 32 * b : 32 * (b + 1)],
                    sums[:, i * P : (i + 1) * P].rearrange("v (q t) -> v t q", t=PACK),
                )

        def whole_block(b, tags, between):
            banks = [bank(2 * b + h) for h in range(T // BANK)]
            for d in range(D):
                if b == 0 and d == 0:
                    gather(b, d, 0, BANK, banks[0:1], tags[d])
                    gather(b, d, BANK, BANK, banks[1:2])
                else:
                    gather(b, d, 0, T, banks, tags[d])
                between[d]()
            for h, sums in enumerate(banks):
                to_mid(b, h * BANK, sums[:])

        def finish(n):
            v0, width = starts[n], CHUNKS[n]
            last = n >= len(CHUNKS) - 2
            o_f = ring.tile([P, PACK, width], F32, name="o_f")
            o_bf = ring.tile([P, width, PACK], BF16, name="o_bf", align_bytes=64)
            for i in range(width // P):
                f_ps = bank(4 + (v0 // P + i) % 4)
                for t in range(PACK):
                    nc.tensor.transpose(f_ps[:, t * P : (t + 1) * P], mids[v0 // P + i][:, t, :], ident[:])
                f_tv = f_ps[:].rearrange("p (t v) -> p t v", t=PACK)
                nc.scalar.copy(o_f[:, :, i * P : (i + 1) * P], f_tv)
                if not last:
                    nc.scalar.copy(o_bf[:, i * P : (i + 1) * P, :], f_tv.rearrange("p t v -> p v t"))
            nc.sync.dma_start(out=out_rows[:, :, v0 : v0 + width], in_=o_f[:])
            if last:
                nc.vector.tensor_copy(o_bf[:], o_f[:].rearrange("p t v -> p v t"))
            for c0 in range(0, width, 2 * P):
                c1 = min(c0 + 2 * P, width)
                nc.vector.quantize_mx(
                    o_q[:, v0 + c0 : v0 + c1].bitcast(FP8X4),
                    o_sc[:, v0 + c0 : v0 + c1],
                    o_bf[:, c0:c1, :].rearrange("p v t -> p (v t)"),
                )
            nc.sync.dma_start(out=out_words[:, v0 : v0 + width], in_=o_q[:, v0 : v0 + width].bitcast(I32))

        spread(0)
        project(0)
        spread(1)
        spread(2)
        whole_block(0, ("stage_2", "stage_3", "stage_1"), (lambda: None, lambda: project(1), lambda: project(2)))
        whole_block(1, ("stage_2", None, "stage_3"), (lambda: None, lambda: project(3), lambda: None))
        for n, width in enumerate(CHUNKS):
            for b in range(2, BLOCKS):
                sums = bank(2 * (n % 2) + b - 2)
                for d in range(D):
                    held = n > 0 and (b, d) == (BLOCKS - 1, D - 1)
                    gather(b, d, starts[n], width, [sums], "mid_%d" % (starts[n - 1] // P) if held else None)
                to_mid(b, starts[n], sums[:, 0:width])
            finish(n)
        for q in range(4):
            queue = nc.sync if q % 2 == 0 else nc.scalar
            queue.dma_start(
                out=out_2[0, 4 * q : 4 * q + 4, :].bitcast(I32),
                in_=o_sc[32 * q : 32 * q + 4, :].bitcast(I32),
            )
